import numpy as np
import ml_dtypes


def mxq(x, axis, fmt="e4m3"):
    dtype, down = {"e4m3": (ml_dtypes.float8_e4m3fn, 7), "e5m2": (ml_dtypes.float8_e5m2, 14)}[fmt]
    v = np.moveaxis(np.asarray(x, np.float32).astype(ml_dtypes.bfloat16).astype(np.float64), axis, -1)
    blocks = v.reshape(v.shape[:-1] + (-1, 32))
    amax = np.abs(blocks).max(-1, keepdims=True)
    byte = np.maximum(np.where(amax > 0, np.frexp(amax)[1] - 1 + 127, 0) - down, 1)
    scale = np.exp2(byte - 127.0)
    codes = (blocks / scale).astype(np.float32).astype(dtype).astype(np.float64)
    return np.moveaxis((codes * scale).reshape(v.shape), -1, axis)


WIDE = False


def mx_kscale(k):
    if not WIDE:
        return np.ones(k)
    levels = np.array([10, -10, 5, -5, 0])
    if k % 512:
        return np.exp2(np.random.permutation(np.resize(levels, k // 32))).repeat(32)
    a = np.empty((k // 512, 16))
    for p in range(k // 512):
        a[p, :8] = np.random.permutation(np.resize(levels, 8))
        for g in range(8):
            far = levels[np.abs(levels - a[p, g]) >= 10]
            a[p, g + 8] = far[np.random.randint(len(far))]
    return np.exp2(a.ravel()).repeat(32)


def f64(x):
    return np.asarray(x).astype(np.float64)


def striped(idx):
    return np.tile(idx.reshape(-1, 16).T, (8, 1)).astype(np.uint16)


def unstriped(offs):
    return offs[:16].T.reshape(-1).astype(np.int64)


def striped8(idx):
    return np.concatenate([x.reshape(-1, 16).T for x in idx]).astype(np.uint16)


def runs(offs, k):
    lists = np.stack([offs[16 * r : 16 * r + 16].T.reshape(-1) for r in range(8)]).astype(np.int64)
    return lists[np.arange(k) % 512 // 64]


def pack_weight(w):
    k, n = w.shape
    w = f64(np.asarray(w, np.float32).astype(ml_dtypes.bfloat16)).reshape(k // 32, 32, n)
    amax = np.abs(w).max(1)
    byte = np.clip(np.where(amax > 0, np.frexp(amax)[1] - 1 + 127 - 7, 1), 1, 254)
    scaled = (w * np.exp2(127.0 - byte)[:, None, :]).reshape(k, n).astype(np.float32)
    words = np.ascontiguousarray(scaled.reshape(k // 512, 128, 4, n).transpose(0, 1, 3, 2)).astype(ml_dtypes.float8_e4m3fn).view(np.uint8)
    return words, np.ascontiguousarray(byte.astype(np.uint8).reshape(k // 512, 16, n))


def unpack_weight(words, scales):
    g, p, n, _ = words.shape
    vals = np.ascontiguousarray(words).view(ml_dtypes.float8_e4m3fn).astype(np.float64) * np.repeat(np.exp2(scales.astype(np.float64) - 127.0), 8, axis=1)[..., None]
    return vals.transpose(0, 1, 3, 2).reshape(g * 512, n)


K, T, S, N, H, J = 512, 2048, 512, 512, 512, 512


def setup_inputs():
    n = np.random.standard_normal
    s = mx_kscale(K)[:, None]
    u = mx_kscale(H)
    packed_xT = pack_weight(n((K, T)) * s)
    return {
        "x_words": packed_xT[0],
        "x_scales": packed_xT[1],
        "w1": (n((K, H)) / np.sqrt(K) / s).astype(np.float32),
        "gn": (np.random.uniform(0.5, 1.5, (H, 1)) * u[:, None]).astype(np.float32),
        "gm": (np.random.uniform(0.5, 1.5, (H, 1)) * u[:, None]).astype(np.float32),
        "w2": (n((H, N)) / np.sqrt(2 * H) / u[:, None]).astype(np.float32),
        "w3": (n((H, N)) / np.sqrt(2 * H) / u[:, None]).astype(np.float32),
        "tab": n((N, J)).astype(np.float32),
        "offs": striped(np.random.permutation(T)[:S]),
        "n1": striped8(np.stack([np.random.permutation(S) for _ in range(8)])),
        "n2": striped8(np.stack([np.random.permutation(S) for _ in range(8)])),
        "n3": striped8(np.stack([np.random.permutation(S) for _ in range(8)])),
        "n4": striped8(np.stack([np.random.permutation(S) for _ in range(8)])),
        "n5": striped8(np.random.randint(0, J, (8, S))),
        "n6": striped8(np.stack([np.random.permutation(S) for _ in range(8)])),
    }


def reference(x_words, x_scales, w1, gn, gm, w2, w3, tab, offs, n1, n2, n3, n4, n5, n6):
    xq = unpack_weight(x_words, x_scales)[:, unstriped(offs)]
    y = mxq(f64(w1), 0, "e4m3").T @ xq
    sq = (y) ** 2
    z = f64(gn) * ((y[np.arange(H)[:, None], runs(n2, H)]) / (np.sqrt(sq + sq[np.arange(H)[:, None], runs(n1, H)] + 0.25)))
    st = np.maximum(y, y[np.arange(H)[:, None], runs(n3, H)])
    z2 = f64(gm) * (st[np.arange(H)[:, None], runs(n4, H)] - (0.5 * y))
    h = mxq(f64(w2), 0, "e4m3").T @ mxq(z, 0, "e4m3") + mxq(f64(w3), 0, "e4m3").T @ mxq(z2, 0, "e4m3")
    return np.abs(h - (h[np.arange(N)[:, None], runs(n6, N)]) - (f64(tab)[np.arange(N)[:, None], runs(n5, N)]))

@@ -1,0 +1,267 @@
+from contextlib import ExitStack
+
+import concourse.mybir as mybir
+
+K, T, S, N, H, J = 512, 2048, 512, 512, 512, 512
+FLOPS = 2 * K * H * S + 2 * 2 * H * N * S
+
+F32 = mybir.dt.float32
+BF16 = mybir.dt.bfloat16
+I32 = mybir.dt.int32
+U32 = mybir.dt.uint32
+U16 = mybir.dt.uint16
+U8 = mybir.dt.uint8
+FP8X4 = mybir.dt.float8_e4m3fn_x4
+ALU = mybir.AluOpType
+ACT = mybir.ActivationFunctionType
+
+P = 128
+PACK = 4
+HALF = S // 2
+HALVES = (0, 1)
+TILES = range(PACK)
+ON_SCALAR = (2, 3)
+PREFETCHED = (0, 1)
+Z_ON_SCALAR = (0, 1, 2, 3)
+COPIED = (1, 2, 3)
+TAIL = (2, 0, 3, 1)
+
+
+def cols(half):
+    return slice(half * HALF, (half + 1) * HALF)
+
+
+def entries(half):
+    return slice(half * HALF // 16, (half + 1) * HALF // 16)
+
+
+def tile_picked_joinrmshopbkindd_none_p_kernel(tc, x_words, x_scales, w1, gn, gm, w2, w3, tab, offs, n1, n2, n3, n4, n5, n6, out):
+    nc = tc.nc
+    with ExitStack() as ctx:
+        lists = ctx.enter_context(tc.tile_pool(name="lists", bufs=1))
+        keep = ctx.enter_context(tc.tile_pool(name="keep", bufs=1))
+        psum = ctx.enter_context(tc.psum_pool(name="psum", bufs=1))
+
+        def load_list(name, source):
+            tile = lists.tile([P, S // 16], U16, name=name)
+            nc.sync.dma_start(tile[:], source)
+            return tile
+
+        def f32_tiles(name, width=S):
+            return [keep.tile([P, width], F32, name="%s%d" % (name, t)) for t in TILES]
+
+        def looked_up(window, offsets, half):
+            return window[:].indirect(offsets[:, entries(half)])
+
+        offs_sb = load_list("offs_sb", offs)
+        table_scales = keep.tile([P, T], U8, name="table_scales")
+        for q in range(4):
+            nc.sync.dma_start(
+                table_scales[32 * q : 32 * q + 32, :].bitcast(I32),
+                x_scales[0, 4 * q : 4 * q + 4, :].bitcast(I32).partition_broadcast(8),
+            )
+        w1_raw = keep.tile([P, PACK, H], F32, name="w1_raw")
+        nc.sync.dma_start(w1_raw[:], w1.rearrange("(p j) c -> p j c", j=PACK))
+        table_words = keep.tile([P, T], U32, name="table_words")
+        nc.sync.dma_start(table_words[:].bitcast(I32), x_words[0].rearrange("p n t -> p (n t)").bitcast(I32))
+        n3_sb = load_list("n3_sb", n3)
+        n4_sb = load_list("n4_sb", n4)
+        n1_sb = load_list("n1_sb", n1)
+        w3_raw = keep.tile([P, PACK, N], F32, name="w3_raw")
+        nc.sync.dma_start(w3_raw[:], w3.rearrange("(p j) c -> p j c", j=PACK))
+        gm_sb = keep.tile([P, PACK], F32, name="gm_sb")
+        nc.sync.dma_start(gm_sb[:], gm.rearrange("(p t) o -> p (t o)", t=PACK))
+        gn_sb = keep.tile([P, PACK], F32, name="gn_sb")
+        nc.sync.dma_start(gn_sb[:], gn.rearrange("(p t) o -> p (t o)", t=PACK))
+        n2_sb = load_list("n2_sb", n2)
+        w2_raw = keep.tile([P, PACK, N], F32, name="w2_raw")
+        nc.sync.dma_start(w2_raw[:], w2.rearrange("(p j) c -> p j c", j=PACK))
+        n5_sb = load_list("n5_sb", n5)
+        n6_sb = load_list("n6_sb", n6)
+        tab_sb = f32_tiles("tab_sb", J)
+        tab_rows = tab.rearrange("(b t q) n -> t b q n", t=PACK, q=8)
+        out_rows = out.rearrange("(b t q) n -> t b q n", t=PACK, q=8)
+        for t in TILES:
+            nc.sync.dma_start(tab_sb[t][:], tab_rows[t])
+
+        picked_scales = keep.tile([P, S], U8, name="picked_scales", align_bytes=64)
+        nc.vector.tensor_copy(picked_scales[:], table_scales[:].indirect(offs_sb[:]))
+
+        w1_bf = keep.tile([P, PACK * H], BF16, name="w1_bf", align_bytes=64)
+        w1_codes = keep.tile([P, H], U32, name="w1_codes", align_bytes=64)
+        w1_scales = keep.tile([P, H], U8, name="w1_scales", align_bytes=64)
+        w1_from = w1_raw[:].rearrange("p j (m t) -> p m j t", t=PACK)
+        w1_to = w1_bf[:].rearrange("p (t m j) -> p m j t", t=PACK, j=PACK)
+        nc.vector.tensor_copy(w1_to[:, :, :, 0:2], w1_from[:, :, :, 0:2])
+        nc.scalar.copy(w1_to[:, :, :, 2:4], w1_from[:, :, :, 2:4])
+        for pair in (0, 1):
+            nc.vector.quantize_mx(
+                w1_codes[:, pair * 256 : (pair + 1) * 256].bitcast(FP8X4),
+                w1_scales[:, pair * 256 : (pair + 1) * 256],
+                w1_bf[:, pair * 1024 : (pair + 1) * 1024],
+            )
+
+        picked_words = [keep.tile([P, HALF], U32, name="picked_words%d" % h, align_bytes=64) for h in HALVES]
+        y_bank = {}
+        for h in HALVES:
+            nc.vector.tensor_copy(picked_words[h][:], looked_up(table_words, offs_sb, h))
+        for t in TILES:
+            for h in HALVES:
+                y_bank[t, h] = psum.tile([P, HALF], F32, name="y_bank", tag="bank%d%d" % (t, h))
+                nc.tensor.matmul_mx(
+                    y_bank[t, h][:],
+                    lhsT=w1_codes[:, t * P : (t + 1) * P].bitcast(FP8X4),
+                    lhsT_scale=w1_scales[:, t * P : (t + 1) * P],
+                    rhs=picked_words[h][:].bitcast(FP8X4),
+                    rhs_scale=picked_scales[:, cols(h)],
+                    start=True,
+                    stop=True,
+                )
+
+        half_y = f32_tiles("half_y")
+        half_y3 = f32_tiles("half_y3")
+        st = f32_tiles("st")
+        sq = f32_tiles("sq")
+        total = f32_tiles("total")
+        root = f32_tiles("root")
+        z_raw = [keep.tile([P, PACK, HALF], F32, name="z_raw%d" % h) for h in HALVES]
+        z2_raw = [keep.tile([P, PACK, HALF], F32, name="z2_raw%d" % h) for h in HALVES]
+
+        def quantised(name, raw, gain):
+            rounded = keep.tile([P, PACK * HALF], BF16, name=name + "_bf", align_bytes=64)
+            codes = keep.tile([P, HALF], U32, name=name + "_codes", align_bytes=64)
+            scales = keep.tile([P, HALF], U8, name=name + "_scales", align_bytes=64)
+            target = rounded[:].rearrange("p (c i t) -> p c t i", i=2, t=PACK)
+            source = raw[:].rearrange("p t (c i) -> p c t i", i=2)
+            if gain is None:
+                nc.vector.tensor_copy(target, source)
+            else:
+                nc.vector.tensor_tensor(target, source, gain[:].unsqueeze(1).unsqueeze(3).to_broadcast([P, HALF // 2, PACK, 2]), ALU.mult)
+            return rounded, codes, scales
+
+        def quantise(parts):
+            rounded, codes, scales = parts
+            nc.vector.quantize_mx(codes[:].bitcast(FP8X4), scales[:], rounded[:])
+
+        def round_weights(name, raw, copy):
+            rounded = keep.tile([P, PACK * N], BF16, name=name + "_bf", align_bytes=64)
+            codes = keep.tile([P, N], U32, name=name + "_codes", align_bytes=64)
+            scales = keep.tile([P, N], U8, name=name + "_scales", align_bytes=64)
+            source = raw[:].rearrange("p j (b t e) -> p j b t e", t=PACK, e=8)
+            for t in TILES:
+                copy(
+                    rounded[:, t * N : (t + 1) * N].rearrange("p (b q i j) -> p b q j i", q=4, i=2, j=PACK),
+                    source[:, :, :, t, :].rearrange("p j b (q i) -> p b q j i", i=2),
+                )
+            return rounded, codes, scales
+
+        sq_copy = f32_tiles("sq_copy")
+        half_y2 = f32_tiles("half_y2")
+        kind = f32_tiles("kind")
+
+        def first_steps(t):
+            for h in HALVES:
+                if t == 0 and h == 1:
+                    nc.vector.tensor_scalar(half_y[t][:, cols(h)], y_bank[t, h][:], 0.5, None, ALU.mult)
+                else:
+                    nc.scalar.activation(half_y[t][:, cols(h)], y_bank[t, h][:], ACT.Copy, scale=0.5)
+            for h in HALVES:
+                if t == 0:
+                    nc.vector.tensor_copy(half_y3[t][:, cols(h)], looked_up(half_y[t], n3_sb, h))
+                else:
+                    nc.scalar.activation(half_y3[t][:, cols(h)], looked_up(half_y[t], n3_sb, h), ACT.Copy)
+            for h in HALVES:
+                nc.scalar.activation(sq[t][:, cols(h)], y_bank[t, h][:], ACT.Square)
+            if t in COPIED:
+                nc.sync.dma_start(sq_copy[t][:], sq[t][:])
+            else:
+                for h in HALVES:
+                    nc.scalar.activation(sq_copy[t][:, cols(h)], looked_up(sq[t], n1_sb, h), ACT.Copy)
+            for h in HALVES:
+                nc.vector.scalar_tensor_tensor(st[t][:, cols(h)], half_y3[t][:, cols(h)], 2.0, y_bank[t, h][:], ALU.mult, ALU.max)
+            for h in HALVES:
+                nc.vector.tensor_tensor(z2_raw[h][:, t, :], looked_up(st[t], n4_sb, h), half_y[t][:, cols(h)], ALU.subtract)
+
+        def root_steps(t):
+            if t in COPIED:
+                for h in HALVES:
+                    nc.vector.tensor_tensor(total[t][:, cols(h)], looked_up(sq[t], n1_sb, h), sq_copy[t][:, cols(h)], ALU.add)
+            else:
+                nc.vector.tensor_tensor(total[t][:], sq[t][:], sq_copy[t][:], ALU.add)
+            nc.scalar.activation(root[t][:], total[t][:], ACT.Abs_reciprocal_sqrt, bias=0.0625, scale=0.25)
+
+        for t in TILES:
+            first_steps(t)
+            if t >= 1:
+                root_steps(t - 1)
+        for t in range(PACK - 1, PACK):
+            root_steps(t)
+        for h in HALVES:
+            for t in TILES:
+                if t in Z_ON_SCALAR:
+                    nc.scalar.activation(half_y2[t][:, cols(h)], looked_up(half_y[t], n2_sb, h), ACT.Copy)
+        z2_q = [quantised("z2_%d" % h, z2_raw[h], gm_sb) for h in HALVES]
+        w3_q = round_weights("w3", w3_raw, nc.vector.tensor_copy)
+        for h in HALVES:
+            quantise(z2_q[h])
+        quantise(w3_q)
+        w2_q = round_weights("w2", w2_raw, nc.scalar.copy)
+        for t in PREFETCHED:
+            for h in HALVES:
+                nc.scalar.activation(kind[t][:, cols(h)], looked_up(tab_sb[t], n5_sb, h), ACT.Copy)
+        quantise(w2_q)
+
+        h_bank = {}
+
+        def second_product(weights, values, t, h, first):
+            if first:
+                h_bank[t, h] = psum.tile([P, HALF], F32, name="h_bank", tag="bank%d%d" % (t, h))
+            nc.tensor.matmul_mx(
+                h_bank[t, h][:],
+                lhsT=weights[1][:, t * P : (t + 1) * P].bitcast(FP8X4),
+                lhsT_scale=weights[2][:, t * P : (t + 1) * P],
+                rhs=values[1][:].bitcast(FP8X4),
+                rhs_scale=values[2][:],
+                start=first,
+                stop=not first,
+            )
+
+        for h in HALVES:
+            for t in TILES:
+                second_product(w3_q, z2_q[h], t, h, True)
+        for h in HALVES:
+            for t in TILES:
+                nc.vector.scalar_tensor_tensor(z_raw[h][:, t, :], half_y2[t][:, cols(h)], gn_sb[:, t : t + 1], root[t][:, cols(h)], ALU.mult, ALU.mult)
+            z_q = quantised("z_%d" % h, z_raw[h], None)
+            quantise(z_q)
+            for t in TAIL:
+                second_product(w2_q, z_q, t, h, False)
+
+        h_sb = f32_tiles("h_sb")
+        near = half_y3
+        far = half_y2
+        diff = total
+        size = sq_copy
+
+        def leave_bank(t, h):
+            nc.scalar.copy(h_sb[t][:, cols(h)], h_bank[t, h][:])
+            if t in PREFETCHED:
+                nc.vector.tensor_tensor(near[t][:, cols(h)], h_bank[t, h][:], kind[t][:, cols(h)], ALU.subtract)
+            else:
+                nc.vector.tensor_tensor(near[t][:, cols(h)], looked_up(tab_sb[t], n5_sb, h), h_sb[t][:, cols(h)], ALU.subtract)
+
+        for t in TAIL:
+            leave_bank(t, 0)
+        for t in TAIL:
+            leave_bank(t, 1)
+        for t in TAIL:
+            op = ALU.subtract if t in PREFETCHED else ALU.add
+            for h in HALVES:
+                if t in ON_SCALAR:
+                    nc.scalar.activation(far[t][:, cols(h)], looked_up(h_sb[t], n6_sb, h), ACT.Copy)
+                    nc.vector.tensor_tensor(diff[t][:, cols(h)], far[t][:, cols(h)], near[t][:, cols(h)], op)
+                else:
+                    nc.vector.tensor_tensor(diff[t][:, cols(h)], looked_up(h_sb[t], n6_sb, h), near[t][:, cols(h)], op)
+            for part in ([cols(0), cols(1)] if t == TAIL[-1] else [slice(0, S)]):
+                nc.scalar.activation(size[t][:, part], diff[t][:, part], ACT.Abs)
+                nc.sync.dma_start(out_rows[t][:, :, part], size[t][:, part])

@@ -20,11 +20,10 @@ PACK = 4
 HALF = S // 2
 HALVES = (0, 1)
 TILES = range(PACK)
-ON_SCALAR = (2, 3)
-PREFETCHED = (0, 1)
-Z_ON_SCALAR = (0, 1, 2, 3)
-COPIED = (1, 2, 3)
-TAIL = (2, 0, 3, 1)
+PREFETCHED = (0, 1, 2, 3)
+ON_SCALAR = (1, 3)
+COPIED = ()
+TAIL = (0, 1, 2, 3)
 
 
 def cols(half):
@@ -50,8 +49,12 @@ def tile_picked_joinrmshopbkindd_none_p_kernel(tc, x_words, x_scales, w1, gn, gm
         def f32_tiles(name, width=S):
             return [keep.tile([P, width], F32, name="%s%d" % (name, t)) for t in TILES]
 
-        def looked_up(window, offsets, half):
-            return window[:].indirect(offsets[:, entries(half)])
+
+        half_y = f32_tiles("half_y", 2 * S)
+        sq = f32_tiles("sq", 2 * S)
+        st = f32_tiles("st", 2 * S)
+        h_sb = f32_tiles("h_sb", 2 * S)
+        tab_sb = f32_tiles("tab_sb", 2 * J)
 
         offs_sb = load_list("offs_sb", offs)
         table_scales = keep.tile([P, T], U8, name="table_scales")
@@ -78,11 +81,10 @@ def tile_picked_joinrmshopbkindd_none_p_kernel(tc, x_words, x_scales, w1, gn, gm
         nc.sync.dma_start(w2_raw[:], w2.rearrange("(p j) c -> p j c", j=PACK))
         n5_sb = load_list("n5_sb", n5)
         n6_sb = load_list("n6_sb", n6)
-        tab_sb = f32_tiles("tab_sb", J)
         tab_rows = tab.rearrange("(b t q) n -> t b q n", t=PACK, q=8)
         out_rows = out.rearrange("(b t q) n -> t b q n", t=PACK, q=8)
         for t in TILES:
-            nc.sync.dma_start(tab_sb[t][:], tab_rows[t])
+            nc.sync.dma_start(tab_sb[t][:, :J], tab_rows[t])
 
         picked_scales = keep.tile([P, S], U8, name="picked_scales", align_bytes=64)
         nc.vector.tensor_copy(picked_scales[:], table_scales[:].indirect(offs_sb[:]))
@@ -101,167 +103,157 @@ def tile_picked_joinrmshopbkindd_none_p_kernel(tc, x_words, x_scales, w1, gn, gm
                 w1_bf[:, pair * 1024 : (pair + 1) * 1024],
             )
 
-        picked_words = [keep.tile([P, HALF], U32, name="picked_words%d" % h, align_bytes=64) for h in HALVES]
-        y_bank = {}
+        picked_words = keep.tile([P, S], U32, name="picked_words", align_bytes=64)
         for h in HALVES:
-            nc.vector.tensor_copy(picked_words[h][:], looked_up(table_words, offs_sb, h))
+            nc.vector.tensor_copy(picked_words[:, cols(h)], table_words[:].indirect(offs_sb[:, entries(h)]))
+
+        def parts(t):
+            return [cols(0), cols(1)] if t < 1 else [slice(0, S)]
+
+        y_bank = {}
         for t in TILES:
-            for h in HALVES:
-                y_bank[t, h] = psum.tile([P, HALF], F32, name="y_bank", tag="bank%d%d" % (t, h))
+            for i, part in enumerate(parts(t)):
+                y_bank[t, i] = psum.tile([P, part.stop - part.start], F32, name="y_bank", tag="bank%d%d" % (t, i))
                 nc.tensor.matmul_mx(
-                    y_bank[t, h][:],
+                    y_bank[t, i][:],
                     lhsT=w1_codes[:, t * P : (t + 1) * P].bitcast(FP8X4),
                     lhsT_scale=w1_scales[:, t * P : (t + 1) * P],
-                    rhs=picked_words[h][:].bitcast(FP8X4),
-                    rhs_scale=picked_scales[:, cols(h)],
+                    rhs=picked_words[:, part].bitcast(FP8X4),
+                    rhs_scale=picked_scales[:, part],
                     start=True,
                     stop=True,
                 )
 
-        half_y = f32_tiles("half_y")
-        half_y3 = f32_tiles("half_y3")
-        st = f32_tiles("st")
-        sq = f32_tiles("sq")
+        other = f32_tiles("other")
         total = f32_tiles("total")
         root = f32_tiles("root")
-        z_raw = [keep.tile([P, PACK, HALF], F32, name="z_raw%d" % h) for h in HALVES]
-        z2_raw = [keep.tile([P, PACK, HALF], F32, name="z2_raw%d" % h) for h in HALVES]
+        z_raw = keep.tile([P, PACK, S], F32, name="z_raw")
+        z2_raw = keep.tile([P, PACK, S], F32, name="z2_raw")
 
-        def quantised(name, raw, gain):
-            rounded = keep.tile([P, PACK * HALF], BF16, name=name + "_bf", align_bytes=64)
-            codes = keep.tile([P, HALF], U32, name=name + "_codes", align_bytes=64)
-            scales = keep.tile([P, HALF], U8, name=name + "_scales", align_bytes=64)
-            target = rounded[:].rearrange("p (c i t) -> p c t i", i=2, t=PACK)
-            source = raw[:].rearrange("p t (c i) -> p c t i", i=2)
-            if gain is None:
-                nc.vector.tensor_copy(target, source)
-            else:
-                nc.vector.tensor_tensor(target, source, gain[:].unsqueeze(1).unsqueeze(3).to_broadcast([P, HALF // 2, PACK, 2]), ALU.mult)
+        def mx_tiles(name, width):
+            rounded = keep.tile([P, PACK * width], BF16, name=name + "_bf", align_bytes=64)
+            codes = keep.tile([P, width], U32, name=name + "_codes", align_bytes=64)
+            scales = keep.tile([P, width], U8, name=name + "_scales", align_bytes=64)
             return rounded, codes, scales
 
-        def quantise(parts):
-            rounded, codes, scales = parts
+        def round_values(name, raw, gain):
+            width = raw.shape[2]
+            tiles = mx_tiles(name, width)
+            nc.vector.tensor_tensor(
+                tiles[0][:].rearrange("p (c i t) -> p c t i", i=2, t=PACK),
+                raw.rearrange("p t (c i) -> p c t i", i=2),
+                gain[:].unsqueeze(1).unsqueeze(3).to_broadcast([P, width // 2, PACK, 2]),
+                ALU.mult,
+            )
+            return tiles
+
+        def quantise(tiles):
+            rounded, codes, scales = tiles
             nc.vector.quantize_mx(codes[:].bitcast(FP8X4), scales[:], rounded[:])
 
-        def round_weights(name, raw, copy):
-            rounded = keep.tile([P, PACK * N], BF16, name=name + "_bf", align_bytes=64)
-            codes = keep.tile([P, N], U32, name=name + "_codes", align_bytes=64)
-            scales = keep.tile([P, N], U8, name=name + "_scales", align_bytes=64)
+        def round_weights(name, raw, on_vector):
+            tiles = mx_tiles(name, N)
             source = raw[:].rearrange("p j (b t e) -> p j b t e", t=PACK, e=8)
             for t in TILES:
+                copy = nc.vector.tensor_copy if t < on_vector else nc.scalar.copy
                 copy(
-                    rounded[:, t * N : (t + 1) * N].rearrange("p (b q i j) -> p b q j i", q=4, i=2, j=PACK),
+                    tiles[0][:, t * N : (t + 1) * N].rearrange("p (b q i j) -> p b q j i", q=4, i=2, j=PACK),
                     source[:, :, :, t, :].rearrange("p j b (q i) -> p b q j i", i=2),
                 )
-            return rounded, codes, scales
-
-        sq_copy = f32_tiles("sq_copy")
-        half_y2 = f32_tiles("half_y2")
-        kind = f32_tiles("kind")
+            return tiles
 
         def first_steps(t):
-            for h in HALVES:
-                if t == 0 and h == 1:
-                    nc.vector.tensor_scalar(half_y[t][:, cols(h)], y_bank[t, h][:], 0.5, None, ALU.mult)
+            for i, part in enumerate(parts(t)):
+                if t == 0 and i == 1:
+                    nc.vector.tensor_scalar(half_y[t][:, part], y_bank[t, i][:], 0.5, None, ALU.mult)
                 else:
-                    nc.scalar.activation(half_y[t][:, cols(h)], y_bank[t, h][:], ACT.Copy, scale=0.5)
-            for h in HALVES:
-                if t == 0:
-                    nc.vector.tensor_copy(half_y3[t][:, cols(h)], looked_up(half_y[t], n3_sb, h))
-                else:
-                    nc.scalar.activation(half_y3[t][:, cols(h)], looked_up(half_y[t], n3_sb, h), ACT.Copy)
-            for h in HALVES:
-                nc.scalar.activation(sq[t][:, cols(h)], y_bank[t, h][:], ACT.Square)
-            if t in COPIED:
-                nc.sync.dma_start(sq_copy[t][:], sq[t][:])
+                    nc.scalar.activation(half_y[t][:, part], y_bank[t, i][:], ACT.Copy, scale=0.5)
+            if t == 0:
+                nc.vector.tensor_copy(st[t][:, S:], half_y[t][:].indirect(n3_sb[:]))
             else:
-                for h in HALVES:
-                    nc.scalar.activation(sq_copy[t][:, cols(h)], looked_up(sq[t], n1_sb, h), ACT.Copy)
-            for h in HALVES:
-                nc.vector.scalar_tensor_tensor(st[t][:, cols(h)], half_y3[t][:, cols(h)], 2.0, y_bank[t, h][:], ALU.mult, ALU.max)
-            for h in HALVES:
-                nc.vector.tensor_tensor(z2_raw[h][:, t, :], looked_up(st[t], n4_sb, h), half_y[t][:, cols(h)], ALU.subtract)
+                nc.scalar.activation(st[t][:, S:], half_y[t][:].indirect(n3_sb[:]), ACT.Copy)
+            for i, part in enumerate(parts(t)):
+                nc.vector.scalar_tensor_tensor(st[t][:, part], st[t][:, S + part.start : S + part.stop], 2.0, y_bank[t, i][:], ALU.mult, ALU.max)
+            nc.vector.tensor_tensor(z2_raw[:, t, :], st[t][:].indirect(n4_sb[:]), half_y[t][:, :S], ALU.subtract)
 
-        def root_steps(t):
+        def square(t):
+            for i, part in enumerate(parts(t)):
+                nc.scalar.activation(sq[t][:, part], y_bank[t, i][:], ACT.Square)
             if t in COPIED:
-                for h in HALVES:
-                    nc.vector.tensor_tensor(total[t][:, cols(h)], looked_up(sq[t], n1_sb, h), sq_copy[t][:, cols(h)], ALU.add)
+                nc.sync.dma_start(other[t][:], sq[t][:, :S])
+
+        def sum_steps(t):
+            if t in COPIED:
+                nc.vector.tensor_tensor(total[t][:], sq[t][:].indirect(n1_sb[:]), other[t][:], ALU.add)
             else:
-                nc.vector.tensor_tensor(total[t][:], sq[t][:], sq_copy[t][:], ALU.add)
+                nc.scalar.activation(other[t][:], sq[t][:].indirect(n1_sb[:]), ACT.Copy)
+                nc.vector.tensor_tensor(total[t][:], sq[t][:, :S], other[t][:], ALU.add)
+
+        def root_step(t):
             nc.scalar.activation(root[t][:], total[t][:], ACT.Abs_reciprocal_sqrt, bias=0.0625, scale=0.25)
-
-        for t in TILES:
-            first_steps(t)
-            if t >= 1:
-                root_steps(t - 1)
-        for t in range(PACK - 1, PACK):
-            root_steps(t)
-        for h in HALVES:
-            for t in TILES:
-                if t in Z_ON_SCALAR:
-                    nc.scalar.activation(half_y2[t][:, cols(h)], looked_up(half_y[t], n2_sb, h), ACT.Copy)
-        z2_q = [quantised("z2_%d" % h, z2_raw[h], gm_sb) for h in HALVES]
-        w3_q = round_weights("w3", w3_raw, nc.vector.tensor_copy)
-        for h in HALVES:
-            quantise(z2_q[h])
-        quantise(w3_q)
-        w2_q = round_weights("w2", w2_raw, nc.scalar.copy)
-        for t in PREFETCHED:
-            for h in HALVES:
-                nc.scalar.activation(kind[t][:, cols(h)], looked_up(tab_sb[t], n5_sb, h), ACT.Copy)
-        quantise(w2_q)
 
         h_bank = {}
 
-        def second_product(weights, values, t, h, first):
+        def second_product(weights, values, part, t, h, first):
             if first:
                 h_bank[t, h] = psum.tile([P, HALF], F32, name="h_bank", tag="bank%d%d" % (t, h))
             nc.tensor.matmul_mx(
                 h_bank[t, h][:],
                 lhsT=weights[1][:, t * P : (t + 1) * P].bitcast(FP8X4),
                 lhsT_scale=weights[2][:, t * P : (t + 1) * P],
-                rhs=values[1][:].bitcast(FP8X4),
-                rhs_scale=values[2][:],
+                rhs=values[1][:, part].bitcast(FP8X4),
+                rhs_scale=values[2][:, part],
                 start=first,
                 stop=not first,
             )
 
+        def fetch_kinds(tiles):
+            for t in tiles:
+                nc.scalar.activation(h_sb[t][:, S:], tab_sb[t][:].indirect(n5_sb[:]), ACT.Copy)
+
+        for t in TILES:
+            first_steps(t)
+        for t in TILES:
+            square(t)
+            sum_steps(t)
+        for t in TILES:
+            root_step(t)
+        z2_q = round_values("z2", z2_raw[:], gm_sb)
+        quantise(z2_q)
+        w3_q = round_weights("w3", w3_raw, 0)
+        w2_q = round_weights("w2", w2_raw, 2)
+        fetch_kinds(PREFETCHED)
+        quantise(w3_q)
+        quantise(w2_q)
         for h in HALVES:
-            for t in TILES:
-                second_product(w3_q, z2_q[h], t, h, True)
+            for t in TAIL:
+                second_product(w3_q, z2_q, cols(h), t, h, True)
+        for t in TILES:
+            nc.vector.tensor_tensor(z_raw[:, t, :], half_y[t][:].indirect(n2_sb[:]), root[t][:], ALU.mult)
+
         for h in HALVES:
-            for t in TILES:
-                nc.vector.scalar_tensor_tensor(z_raw[h][:, t, :], half_y2[t][:, cols(h)], gn_sb[:, t : t + 1], root[t][:, cols(h)], ALU.mult, ALU.mult)
-            z_q = quantised("z_%d" % h, z_raw[h], None)
+            z_q = round_values("z_%d" % h, z_raw[:, :, cols(h)], gn_sb)
             quantise(z_q)
             for t in TAIL:
-                second_product(w2_q, z_q, t, h, False)
+                second_product(w2_q, z_q, slice(0, HALF), t, h, False)
 
-        h_sb = f32_tiles("h_sb")
-        near = half_y3
-        far = half_y2
+        near = other
+        far = root
         diff = total
-        size = sq_copy
-
-        def leave_bank(t, h):
-            nc.scalar.copy(h_sb[t][:, cols(h)], h_bank[t, h][:])
-            if t in PREFETCHED:
-                nc.vector.tensor_tensor(near[t][:, cols(h)], h_bank[t, h][:], kind[t][:, cols(h)], ALU.subtract)
-            else:
-                nc.vector.tensor_tensor(near[t][:, cols(h)], looked_up(tab_sb[t], n5_sb, h), h_sb[t][:, cols(h)], ALU.subtract)
-
-        for t in TAIL:
-            leave_bank(t, 0)
-        for t in TAIL:
-            leave_bank(t, 1)
+        for h in HALVES:
+            for t in TAIL:
+                nc.scalar.copy(h_sb[t][:, cols(h)], h_bank[t, h][:])
+                if t in PREFETCHED:
+                    nc.vector.tensor_tensor(near[t][:, cols(h)], h_bank[t, h][:], h_sb[t][:, S + h * HALF : S + (h + 1) * HALF], ALU.subtract)
+                else:
+                    nc.vector.tensor_tensor(near[t][:, cols(h)], tab_sb[t][:].indirect(n5_sb[:, entries(h)]), h_sb[t][:, cols(h)], ALU.subtract)
         for t in TAIL:
             op = ALU.subtract if t in PREFETCHED else ALU.add
-            for h in HALVES:
-                if t in ON_SCALAR:
-                    nc.scalar.activation(far[t][:, cols(h)], looked_up(h_sb[t], n6_sb, h), ACT.Copy)
-                    nc.vector.tensor_tensor(diff[t][:, cols(h)], far[t][:, cols(h)], near[t][:, cols(h)], op)
-                else:
-                    nc.vector.tensor_tensor(diff[t][:, cols(h)], looked_up(h_sb[t], n6_sb, h), near[t][:, cols(h)], op)
+            if t in ON_SCALAR:
+                nc.scalar.activation(far[t][:], h_sb[t][:].indirect(n6_sb[:]), ACT.Copy)
+                nc.vector.tensor_tensor(diff[t][:], far[t][:], near[t][:], op)
+            else:
+                nc.vector.tensor_tensor(diff[t][:], h_sb[t][:].indirect(n6_sb[:]), near[t][:], op)
             for part in ([cols(0), cols(1)] if t == TAIL[-1] else [slice(0, S)]):
-                nc.scalar.activation(size[t][:, part], diff[t][:, part], ACT.Abs)
-                nc.sync.dma_start(out_rows[t][:, :, part], size[t][:, part])
+                nc.scalar.activation(z_raw[:, t, part], diff[t][:, part], ACT.Abs)
+                nc.sync.dma_start(out_rows[t][:, :, part], z_raw[:, t, part])

@@ -49,6 +49,9 @@ def tile_picked_joinrmshopbkindd_none_p_kernel(tc, x_words, x_scales, w1, gn, gm
         def f32_tiles(name, width=S):
             return [keep.tile([P, width], F32, name="%s%d" % (name, t)) for t in TILES]
 
+        warm = keep.tile([P, 2], F32, name="warm")
+        nc.vector.memset(warm[:, 0:1], 1.0)
+        nc.scalar.activation(warm[:, 1:2], warm[:, 0:1], ACT.Abs_reciprocal_sqrt)
 
         half_y = f32_tiles("half_y", 2 * S)
         sq = f32_tiles("sq", 2 * S)

@@ -1,6 +1,7 @@
 from contextlib import ExitStack
 
 import concourse.mybir as mybir
+from concourse.masks import make_identity
 
 K, T, S, N, H, J = 512, 2048, 512, 512, 512, 512
 FLOPS = 2 * K * H * S + 2 * 2 * H * N * S
@@ -23,6 +24,8 @@ TILES = range(PACK)
 PREFETCHED = (0, 1, 2, 3)
 ON_SCALAR = (1, 3)
 COPIED = ()
+KIND_ON_VECTOR = ()
+N3_ON_VECTOR = (0, 1)
 TAIL = (0, 1, 2, 3)
 
 
@@ -59,6 +62,9 @@ def tile_picked_joinrmshopbkindd_none_p_kernel(tc, x_words, x_scales, w1, gn, gm
         h_sb = f32_tiles("h_sb", 2 * S)
         tab_sb = f32_tiles("tab_sb", 2 * J)
 
+        identity = keep.tile([P, P], F32, name="identity")
+        make_identity(nc, identity[:])
+
         offs_sb = load_list("offs_sb", offs)
         table_scales = keep.tile([P, T], U8, name="table_scales")
         for q in range(4):
@@ -89,9 +95,6 @@ def tile_picked_joinrmshopbkindd_none_p_kernel(tc, x_words, x_scales, w1, gn, gm
         for t in TILES:
             nc.sync.dma_start(tab_sb[t][:, :J], tab_rows[t])
 
-        picked_scales = keep.tile([P, S], U8, name="picked_scales", align_bytes=64)
-        nc.vector.tensor_copy(picked_scales[:], table_scales[:].indirect(offs_sb[:]))
-
         w1_bf = keep.tile([P, PACK * H], BF16, name="w1_bf", align_bytes=64)
         w1_codes = keep.tile([P, H], U32, name="w1_codes", align_bytes=64)
         w1_scales = keep.tile([P, H], U8, name="w1_scales", align_bytes=64)
@@ -99,6 +102,8 @@ def tile_picked_joinrmshopbkindd_none_p_kernel(tc, x_words, x_scales, w1, gn, gm
         w1_to = w1_bf[:].rearrange("p (t m j) -> p m j t", t=PACK, j=PACK)
         nc.vector.tensor_copy(w1_to[:, :, :, 0:2], w1_from[:, :, :, 0:2])
         nc.scalar.copy(w1_to[:, :, :, 2:4], w1_from[:, :, :, 2:4])
+        picked_scales = keep.tile([P, S], U8, name="picked_scales", align_bytes=64)
+        nc.vector.tensor_copy(picked_scales[:], table_scales[:].indirect(offs_sb[:]))
         for pair in (0, 1):
             nc.vector.quantize_mx(
                 w1_codes[:, pair * 256 : (pair + 1) * 256].bitcast(FP8X4),
@@ -142,12 +147,12 @@ def tile_picked_joinrmshopbkindd_none_p_kernel(tc, x_words, x_scales, w1, gn, gm
         def round_values(name, raw, gain):
             width = raw.shape[2]
             tiles = mx_tiles(name, width)
-            nc.vector.tensor_tensor(
-                tiles[0][:].rearrange("p (c i t) -> p c t i", i=2, t=PACK),
-                raw.rearrange("p t (c i) -> p c t i", i=2),
-                gain[:].unsqueeze(1).unsqueeze(3).to_broadcast([P, width // 2, PACK, 2]),
-                ALU.mult,
-            )
+            target = tiles[0][:].rearrange("p (c i t) -> p c t i", i=2, t=PACK)
+            source = raw.rearrange("p t (c i) -> p c t i", i=2)
+            if gain is None:
+                nc.vector.tensor_copy(target, source)
+            else:
+                nc.vector.tensor_tensor(target, source, gain[:].unsqueeze(1).unsqueeze(3).to_broadcast([P, width // 2, PACK, 2]), ALU.mult)
             return tiles
 
         def quantise(tiles):
@@ -171,8 +176,9 @@ def tile_picked_joinrmshopbkindd_none_p_kernel(tc, x_words, x_scales, w1, gn, gm
                     nc.vector.tensor_scalar(half_y[t][:, part], y_bank[t, i][:], 0.5, None, ALU.mult)
                 else:
                     nc.scalar.activation(half_y[t][:, part], y_bank[t, i][:], ACT.Copy, scale=0.5)
-            if t == 0:
-                nc.vector.tensor_copy(st[t][:, S:], half_y[t][:].indirect(n3_sb[:]))
+            if t in N3_ON_VECTOR:
+                for h in HALVES:
+                    nc.vector.tensor_copy(st[t][:, S + h * HALF : S + (h + 1) * HALF], half_y[t][:].indirect(n3_sb[:, entries(h)]))
             else:
                 nc.scalar.activation(st[t][:, S:], half_y[t][:].indirect(n3_sb[:]), ACT.Copy)
             for i, part in enumerate(parts(t)):
@@ -185,15 +191,27 @@ def tile_picked_joinrmshopbkindd_none_p_kernel(tc, x_words, x_scales, w1, gn, gm
             if t in COPIED:
                 nc.sync.dma_start(other[t][:], sq[t][:, :S])
 
+        sum_bank = {}
+
         def sum_steps(t):
-            if t in COPIED:
-                nc.vector.tensor_tensor(total[t][:], sq[t][:].indirect(n1_sb[:]), other[t][:], ALU.add)
-            else:
-                nc.scalar.activation(other[t][:], sq[t][:].indirect(n1_sb[:]), ACT.Copy)
-                nc.vector.tensor_tensor(total[t][:], sq[t][:, :S], other[t][:], ALU.add)
+            nc.scalar.activation(other[t][:], sq[t][:].indirect(n1_sb[:]), ACT.Copy)
+            sum_bank[t] = psum.tile([P, S], F32, name="sum_bank", tag="bank%d1" % (1 + t % 2))
+            for b in range(S // P):
+                block = slice(b * P, (b + 1) * P)
+                nc.tensor.matmul(sum_bank[t][:, block], lhsT=sq[t][:, block], rhs=identity[:], start=True, stop=False, is_transpose=True)
+                nc.tensor.matmul(sum_bank[t][:, block], lhsT=other[t][:, block], rhs=identity[:], start=False, stop=True, is_transpose=True)
+
+        root_bank = {}
 
         def root_step(t):
-            nc.scalar.activation(root[t][:], total[t][:], ACT.Abs_reciprocal_sqrt, bias=0.0625, scale=0.25)
+            nc.scalar.activation(total[t][:], sum_bank[t][:], ACT.Abs_reciprocal_sqrt, bias=0.0625, scale=0.25)
+            root_bank[t] = psum.tile([P, S], F32, name="root_bank", tag="bank%d1" % (3 - 3 * (t % 2)))
+            for b in range(S // P):
+                block = slice(b * P, (b + 1) * P)
+                nc.tensor.transpose(root_bank[t][:, block], total[t][:, block], identity[:])
+
+        def gain_step(t):
+            nc.scalar.activation(root[t][:], root_bank[t][:], ACT.Copy, scale=gn_sb[:, t : t + 1])
 
         h_bank = {}
 
@@ -210,24 +228,32 @@ def tile_picked_joinrmshopbkindd_none_p_kernel(tc, x_words, x_scales, w1, gn, gm
                 stop=not first,
             )
 
+        kind = total
+
         def fetch_kinds(tiles):
             for t in tiles:
-                nc.scalar.activation(h_sb[t][:, S:], tab_sb[t][:].indirect(n5_sb[:]), ACT.Copy)
+                if t in KIND_ON_VECTOR:
+                    nc.vector.tensor_copy(kind[t][:], tab_sb[t][:].indirect(n5_sb[:]))
+                else:
+                    nc.scalar.activation(kind[t][:], tab_sb[t][:].indirect(n5_sb[:]), ACT.Copy)
 
         for t in TILES:
             first_steps(t)
-        for t in TILES:
-            square(t)
-            sum_steps(t)
-        for t in TILES:
-            root_step(t)
+        for step in range(PACK + 2):
+            if step < PACK:
+                square(step)
+                sum_steps(step)
+            if 1 <= step < PACK + 1:
+                root_step(step - 1)
+            if 2 <= step:
+                gain_step(step - 2)
         z2_q = round_values("z2", z2_raw[:], gm_sb)
         quantise(z2_q)
-        w3_q = round_weights("w3", w3_raw, 0)
-        w2_q = round_weights("w2", w2_raw, 2)
-        fetch_kinds(PREFETCHED)
+        w3_q = round_weights("w3", w3_raw, 4)
         quantise(w3_q)
+        w2_q = round_weights("w2", w2_raw, 2)
         quantise(w2_q)
+        fetch_kinds(PREFETCHED)
         for h in HALVES:
             for t in TAIL:
                 second_product(w3_q, z2_q, cols(h), t, h, True)
@@ -235,28 +261,33 @@ def tile_picked_joinrmshopbkindd_none_p_kernel(tc, x_words, x_scales, w1, gn, gm
             nc.vector.tensor_tensor(z_raw[:, t, :], half_y[t][:].indirect(n2_sb[:]), root[t][:], ALU.mult)
 
         for h in HALVES:
-            z_q = round_values("z_%d" % h, z_raw[:, :, cols(h)], gn_sb)
+            z_q = round_values("z_%d" % h, z_raw[:, :, cols(h)], None)
             quantise(z_q)
             for t in TAIL:
                 second_product(w2_q, z_q, slice(0, HALF), t, h, False)
 
-        near = other
+        near = f32_tiles("near")
         far = root
-        diff = total
-        for h in HALVES:
-            for t in TAIL:
-                nc.scalar.copy(h_sb[t][:, cols(h)], h_bank[t, h][:])
-                if t in PREFETCHED:
-                    nc.vector.tensor_tensor(near[t][:, cols(h)], h_bank[t, h][:], h_sb[t][:, S + h * HALF : S + (h + 1) * HALF], ALU.subtract)
-                else:
-                    nc.vector.tensor_tensor(near[t][:, cols(h)], tab_sb[t][:].indirect(n5_sb[:, entries(h)]), h_sb[t][:, cols(h)], ALU.subtract)
+        diff = [tile[:, :S] for tile in st]
+
+        def leave_bank(t, h):
+            nc.scalar.copy(h_sb[t][:, cols(h)], h_bank[t, h][:])
+            if t in PREFETCHED:
+                nc.vector.tensor_tensor(near[t][:, cols(h)], h_bank[t, h][:], kind[t][:, cols(h)], ALU.subtract)
+            else:
+                nc.vector.tensor_tensor(near[t][:, cols(h)], tab_sb[t][:].indirect(n5_sb[:, entries(h)]), h_sb[t][:, cols(h)], ALU.subtract)
+
         for t in TAIL:
+            leave_bank(t, 0)
+        for t in TAIL:
+            leave_bank(t, 1)
             op = ALU.subtract if t in PREFETCHED else ALU.add
             if t in ON_SCALAR:
                 nc.scalar.activation(far[t][:], h_sb[t][:].indirect(n6_sb[:]), ACT.Copy)
                 nc.vector.tensor_tensor(diff[t][:], far[t][:], near[t][:], op)
             else:
                 nc.vector.tensor_tensor(diff[t][:], h_sb[t][:].indirect(n6_sb[:]), near[t][:], op)
+        for t in TAIL:
             for part in ([cols(0), cols(1)] if t == TAIL[-1] else [slice(0, S)]):
                 nc.scalar.activation(z_raw[:, t, part], diff[t][:, part], ACT.Abs)
                 nc.sync.dma_start(out_rows[t][:, :, part], z_raw[:, t, part])

from contextlib import ExitStack

import concourse.mybir as mybir
from concourse.masks import make_identity

K, T, S, N, H, J = 512, 2048, 512, 512, 512, 512
FLOPS = 2 * K * H * S + 2 * 2 * H * N * S

F32 = mybir.dt.float32
BF16 = mybir.dt.bfloat16
I32 = mybir.dt.int32
U32 = mybir.dt.uint32
U16 = mybir.dt.uint16
U8 = mybir.dt.uint8
FP8X4 = mybir.dt.float8_e4m3fn_x4
ALU = mybir.AluOpType
ACT = mybir.ActivationFunctionType

P = 128
PACK = 4
HALF = S // 2
HALVES = (0, 1)
TILES = range(PACK)
PREFETCHED = (0, 1, 2, 3)
ON_SCALAR = (1, 3)
COPIED = ()
KIND_ON_VECTOR = ()
N3_ON_VECTOR = (0, 1)
TAIL = (0, 1, 2, 3)


def cols(half):
    return slice(half * HALF, (half + 1) * HALF)


def entries(half):
    return slice(half * HALF // 16, (half + 1) * HALF // 16)


def tile_picked_joinrmshopbkindd_none_p_kernel(tc, x_words, x_scales, w1, gn, gm, w2, w3, tab, offs, n1, n2, n3, n4, n5, n6, out):
    nc = tc.nc
    with ExitStack() as ctx:
        lists = ctx.enter_context(tc.tile_pool(name="lists", bufs=1))
        keep = ctx.enter_context(tc.tile_pool(name="keep", bufs=1))
        psum = ctx.enter_context(tc.psum_pool(name="psum", bufs=1))

        def load_list(name, source):
            tile = lists.tile([P, S // 16], U16, name=name)
            nc.sync.dma_start(tile[:], source)
            return tile

        def f32_tiles(name, width=S):
            return [keep.tile([P, width], F32, name="%s%d" % (name, t)) for t in TILES]

        warm = keep.tile([P, 2], F32, name="warm")
        nc.vector.memset(warm[:, 0:1], 1.0)
        nc.scalar.activation(warm[:, 1:2], warm[:, 0:1], ACT.Abs_reciprocal_sqrt)

        half_y = f32_tiles("half_y", 2 * S)
        sq = f32_tiles("sq", 2 * S)
        st = f32_tiles("st", 2 * S)
        h_sb = f32_tiles("h_sb", 2 * S)
        tab_sb = f32_tiles("tab_sb", 2 * J)

        identity = keep.tile([P, P], F32, name="identity")
        make_identity(nc, identity[:])

        offs_sb = load_list("offs_sb", offs)
        table_scales = keep.tile([P, T], U8, name="table_scales")
        for q in range(4):
            nc.sync.dma_start(
                table_scales[32 * q : 32 * q + 32, :].bitcast(I32),
                x_scales[0, 4 * q : 4 * q + 4, :].bitcast(I32).partition_broadcast(8),
            )
        w1_raw = keep.tile([P, PACK, H], F32, name="w1_raw")
        nc.sync.dma_start(w1_raw[:], w1.rearrange("(p j) c -> p j c", j=PACK))
        table_words = keep.tile([P, T], U32, name="table_words")
        nc.sync.dma_start(table_words[:].bitcast(I32), x_words[0].rearrange("p n t -> p (n t)").bitcast(I32))
        n3_sb = load_list("n3_sb", n3)
        n4_sb = load_list("n4_sb", n4)
        n1_sb = load_list("n1_sb", n1)
        w3_raw = keep.tile([P, PACK, N], F32, name="w3_raw")
        nc.sync.dma_start(w3_raw[:], w3.rearrange("(p j) c -> p j c", j=PACK))
        gm_sb = keep.tile([P, PACK], F32, name="gm_sb")
        nc.sync.dma_start(gm_sb[:], gm.rearrange("(p t) o -> p (t o)", t=PACK))
        gn_sb = keep.tile([P, PACK], F32, name="gn_sb")
        nc.sync.dma_start(gn_sb[:], gn.rearrange("(p t) o -> p (t o)", t=PACK))
        n2_sb = load_list("n2_sb", n2)
        w2_raw = keep.tile([P, PACK, N], F32, name="w2_raw")
        nc.sync.dma_start(w2_raw[:], w2.rearrange("(p j) c -> p j c", j=PACK))
        n5_sb = load_list("n5_sb", n5)
        n6_sb = load_list("n6_sb", n6)
        tab_rows = tab.rearrange("(b t q) n -> t b q n", t=PACK, q=8)
        out_rows = out.rearrange("(b t q) n -> t b q n", t=PACK, q=8)
        for t in TILES:
            nc.sync.dma_start(tab_sb[t][:, :J], tab_rows[t])

        w1_bf = keep.tile([P, PACK * H], BF16, name="w1_bf", align_bytes=64)
        w1_codes = keep.tile([P, H], U32, name="w1_codes", align_bytes=64)
        w1_scales = keep.tile([P, H], U8, name="w1_scales", align_bytes=64)
        w1_from = w1_raw[:].rearrange("p j (m t) -> p m j t", t=PACK)
        w1_to = w1_bf[:].rearrange("p (t m j) -> p m j t", t=PACK, j=PACK)
        nc.vector.tensor_copy(w1_to[:, :, :, 0:2], w1_from[:, :, :, 0:2])
        nc.scalar.copy(w1_to[:, :, :, 2:4], w1_from[:, :, :, 2:4])
        picked_scales = keep.tile([P, S], U8, name="picked_scales", align_bytes=64)
        nc.vector.tensor_copy(picked_scales[:], table_scales[:].indirect(offs_sb[:]))
        for pair in (0, 1):
            nc.vector.quantize_mx(
                w1_codes[:, pair * 256 : (pair + 1) * 256].bitcast(FP8X4),
                w1_scales[:, pair * 256 : (pair + 1) * 256],
                w1_bf[:, pair * 1024 : (pair + 1) * 1024],
            )

        picked_words = keep.tile([P, S], U32, name="picked_words", align_bytes=64)
        for h in HALVES:
            nc.vector.tensor_copy(picked_words[:, cols(h)], table_words[:].indirect(offs_sb[:, entries(h)]))

        def parts(t):
            return [cols(0), cols(1)] if t < 1 else [slice(0, S)]

        y_bank = {}
        for t in TILES:
            for i, part in enumerate(parts(t)):
                y_bank[t, i] = psum.tile([P, part.stop - part.start], F32, name="y_bank", tag="bank%d%d" % (t, i))
                nc.tensor.matmul_mx(
                    y_bank[t, i][:],
                    lhsT=w1_codes[:, t * P : (t + 1) * P].bitcast(FP8X4),
                    lhsT_scale=w1_scales[:, t * P : (t + 1) * P],
                    rhs=picked_words[:, part].bitcast(FP8X4),
                    rhs_scale=picked_scales[:, part],
                    start=True,
                    stop=True,
                )

        other = f32_tiles("other")
        total = f32_tiles("total")
        root = f32_tiles("root")
        z_raw = keep.tile([P, PACK, S], F32, name="z_raw")
        z2_raw = keep.tile([P, PACK, S], F32, name="z2_raw")

        def mx_tiles(name, width):
            rounded = keep.tile([P, PACK * width], BF16, name=name + "_bf", align_bytes=64)
            codes = keep.tile([P, width], U32, name=name + "_codes", align_bytes=64)
            scales = keep.tile([P, width], U8, name=name + "_scales", align_bytes=64)
            return rounded, codes, scales

        def round_values(name, raw, gain):
            width = raw.shape[2]
            tiles = mx_tiles(name, width)
            target = tiles[0][:].rearrange("p (c i t) -> p c t i", i=2, t=PACK)
            source = raw.rearrange("p t (c i) -> p c t i", i=2)
            if gain is None:
                nc.vector.tensor_copy(target, source)
            else:
                nc.vector.tensor_tensor(target, source, gain[:].unsqueeze(1).unsqueeze(3).to_broadcast([P, width // 2, PACK, 2]), ALU.mult)
            return tiles

        def quantise(tiles):
            rounded, codes, scales = tiles
            nc.vector.quantize_mx(codes[:].bitcast(FP8X4), scales[:], rounded[:])

        def round_weights(name, raw, on_vector):
            tiles = mx_tiles(name, N)
            source = raw[:].rearrange("p j (b t e) -> p j b t e", t=PACK, e=8)
            for t in TILES:
                copy = nc.vector.tensor_copy if t < on_vector else nc.scalar.copy
                copy(
                    tiles[0][:, t * N : (t + 1) * N].rearrange("p (b q i j) -> p b q j i", q=4, i=2, j=PACK),
                    source[:, :, :, t, :].rearrange("p j b (q i) -> p b q j i", i=2),
                )
            return tiles

        def first_steps(t):
            for i, part in enumerate(parts(t)):
                if t == 0 and i == 1:
                    nc.vector.tensor_scalar(half_y[t][:, part], y_bank[t, i][:], 0.5, None, ALU.mult)
                else:
                    nc.scalar.activation(half_y[t][:, part], y_bank[t, i][:], ACT.Copy, scale=0.5)
            if t in N3_ON_VECTOR:
                for h in HALVES:
                    nc.vector.tensor_copy(st[t][:, S + h * HALF : S + (h + 1) * HALF], half_y[t][:].indirect(n3_sb[:, entries(h)]))
            else:
                nc.scalar.activation(st[t][:, S:], half_y[t][:].indirect(n3_sb[:]), ACT.Copy)
            for i, part in enumerate(parts(t)):
                nc.vector.scalar_tensor_tensor(st[t][:, part], st[t][:, S + part.start : S + part.stop], 2.0, y_bank[t, i][:], ALU.mult, ALU.max)
            nc.vector.tensor_tensor(z2_raw[:, t, :], st[t][:].indirect(n4_sb[:]), half_y[t][:, :S], ALU.subtract)

        def square(t):
            for i, part in enumerate(parts(t)):
                nc.scalar.activation(sq[t][:, part], y_bank[t, i][:], ACT.Square)
            if t in COPIED:
                nc.sync.dma_start(other[t][:], sq[t][:, :S])

        sum_bank = {}

        def sum_steps(t):
            nc.scalar.activation(other[t][:], sq[t][:].indirect(n1_sb[:]), ACT.Copy)
            sum_bank[t] = psum.tile([P, S], F32, name="sum_bank", tag="bank%d1" % (1 + t % 2))
            for b in range(S // P):
                block = slice(b * P, (b + 1) * P)
                nc.tensor.matmul(sum_bank[t][:, block], lhsT=sq[t][:, block], rhs=identity[:], start=True, stop=False, is_transpose=True)
                nc.tensor.matmul(sum_bank[t][:, block], lhsT=other[t][:, block], rhs=identity[:], start=False, stop=True, is_transpose=True)

        root_bank = {}

        def root_step(t):
            nc.scalar.activation(total[t][:], sum_bank[t][:], ACT.Abs_reciprocal_sqrt, bias=0.0625, scale=0.25)
            root_bank[t] = psum.tile([P, S], F32, name="root_bank", tag="bank%d1" % (3 - 3 * (t % 2)))
            for b in range(S // P):
                block = slice(b * P, (b + 1) * P)
                nc.tensor.transpose(root_bank[t][:, block], total[t][:, block], identity[:])

        def gain_step(t):
            nc.scalar.activation(root[t][:], root_bank[t][:], ACT.Copy, scale=gn_sb[:, t : t + 1])

        h_bank = {}

        def second_product(weights, values, part, t, h, first):
            if first:
                h_bank[t, h] = psum.tile([P, HALF], F32, name="h_bank", tag="bank%d%d" % (t, h))
            nc.tensor.matmul_mx(
                h_bank[t, h][:],
                lhsT=weights[1][:, t * P : (t + 1) * P].bitcast(FP8X4),
                lhsT_scale=weights[2][:, t * P : (t + 1) * P],
                rhs=values[1][:, part].bitcast(FP8X4),
                rhs_scale=values[2][:, part],
                start=first,
                stop=not first,
            )

        kind = total

        def fetch_kinds(tiles):
            for t in tiles:
                if t in KIND_ON_VECTOR:
                    nc.vector.tensor_copy(kind[t][:], tab_sb[t][:].indirect(n5_sb[:]))
                else:
                    nc.scalar.activation(kind[t][:], tab_sb[t][:].indirect(n5_sb[:]), ACT.Copy)

        for t in TILES:
            first_steps(t)
        for step in range(PACK + 2):
            if step < PACK:
                square(step)
                sum_steps(step)
            if 1 <= step < PACK + 1:
                root_step(step - 1)
            if 2 <= step:
                gain_step(step - 2)
        z2_q = round_values("z2", z2_raw[:], gm_sb)
        quantise(z2_q)
        w3_q = round_weights("w3", w3_raw, 4)
        quantise(w3_q)
        w2_q = round_weights("w2", w2_raw, 2)
        quantise(w2_q)
        fetch_kinds(PREFETCHED)
        for h in HALVES:
            for t in TAIL:
                second_product(w3_q, z2_q, cols(h), t, h, True)
        for t in TILES:
            nc.vector.tensor_tensor(z_raw[:, t, :], half_y[t][:].indirect(n2_sb[:]), root[t][:], ALU.mult)

        for h in HALVES:
            z_q = round_values("z_%d" % h, z_raw[:, :, cols(h)], None)
            quantise(z_q)
            for t in TAIL:
                second_product(w2_q, z_q, slice(0, HALF), t, h, False)

        near = f32_tiles("near")
        far = root
        diff = [tile[:, :S] for tile in st]

        def leave_bank(t, h):
            nc.scalar.copy(h_sb[t][:, cols(h)], h_bank[t, h][:])
            if t in PREFETCHED:
                nc.vector.tensor_tensor(near[t][:, cols(h)], h_bank[t, h][:], kind[t][:, cols(h)], ALU.subtract)
            else:
                nc.vector.tensor_tensor(near[t][:, cols(h)], tab_sb[t][:].indirect(n5_sb[:, entries(h)]), h_sb[t][:, cols(h)], ALU.subtract)

        for t in TAIL:
            leave_bank(t, 0)
        for t in TAIL:
            leave_bank(t, 1)
            op = ALU.subtract if t in PREFETCHED else ALU.add
            if t in ON_SCALAR:
                nc.scalar.activation(far[t][:], h_sb[t][:].indirect(n6_sb[:]), ACT.Copy)
                nc.vector.tensor_tensor(diff[t][:], far[t][:], near[t][:], op)
            else:
                nc.vector.tensor_tensor(diff[t][:], h_sb[t][:].indirect(n6_sb[:]), near[t][:], op)
        for t in TAIL:
            for part in ([cols(0), cols(1)] if t == TAIL[-1] else [slice(0, S)]):
                nc.scalar.activation(z_raw[:, t, part], diff[t][:, part], ACT.Abs)
                nc.sync.dma_start(out_rows[t][:, :, part], z_raw[:, t, part])
